import numpy as np
import ml_dtypes


def mxq(x, axis, fmt="e4m3"):
    dtype, down = {"e4m3": (ml_dtypes.float8_e4m3fn, 7), "e5m2": (ml_dtypes.float8_e5m2, 14)}[fmt]
    v = np.moveaxis(np.asarray(x, np.float32).astype(ml_dtypes.bfloat16).astype(np.float64), axis, -1)
    blocks = v.reshape(v.shape[:-1] + (-1, 32))
    amax = np.abs(blocks).max(-1, keepdims=True)
    byte = np.maximum(np.where(amax > 0, np.frexp(amax)[1] - 1 + 127, 0) - down, 1)
    scale = np.exp2(byte - 127.0)
    codes = (blocks / scale).astype(np.float32).astype(dtype).astype(np.float64)
    return np.moveaxis((codes * scale).reshape(v.shape), -1, axis)


WIDE = False


def mx_kscale(k):
    if not WIDE:
        return np.ones(k)
    levels = np.array([10, -10, 5, -5, 0])
    if k % 512:
        return np.exp2(np.random.permutation(np.resize(levels, k // 32))).repeat(32)
    a = np.empty((k // 512, 16))
    for p in range(k // 512):
        a[p, :8] = np.random.permutation(np.resize(levels, 8))
        for g in range(8):
            far = levels[np.abs(levels - a[p, g]) >= 10]
            a[p, g + 8] = far[np.random.randint(len(far))]
    return np.exp2(a.ravel()).repeat(32)


def f64(x):
    return np.asarray(x).astype(np.float64)


def striped(idx):
    return np.tile(np.asarray(idx).reshape(-1, 16).T, (8, 1)).astype(np.uint16)


def unstriped(offs):
    return offs[:16].T.reshape(-1).astype(np.int64)


E2M1 = np.array([0.0, 0.5, 1.0, 1.5, 2.0, 3.0, 4.0, 6.0, -0.0, -0.5, -1.0, -1.5, -2.0, -3.0, -4.0, -6.0])


def pack_weight(w, fmt):
    k, n = w.shape
    w = f64(np.asarray(w, np.float32).astype(ml_dtypes.bfloat16)).reshape(k // 32, 32, n)
    amax = np.abs(w).max(1)
    if fmt == "e4m3":
        byte = np.frexp(amax)[1] - 1 + 127 - 7
    else:
        mant, ex = np.frexp(amax / 6.0)
        byte = np.where(mant > 0.5, ex, ex - 1) + 127
    byte = np.clip(np.where(amax > 0, byte, 1), 1, 254)
    scaled = (w * np.exp2(127.0 - byte)[:, None, :]).reshape(k, n).astype(np.float32)
    by_word = np.ascontiguousarray(scaled.reshape(k // 512, 128, 4, n).transpose(0, 1, 3, 2))
    if fmt == "e4m3":
        words = by_word.astype(ml_dtypes.float8_e4m3fn).view(np.uint8)
    else:
        c = by_word.astype(ml_dtypes.float4_e2m1fn).view(np.uint8) & 0xF
        words = (c[..., 0::2] | (c[..., 1::2] << 4)).reshape(k // 512, 128, 2 * n)
    return np.ascontiguousarray(words), np.ascontiguousarray(byte.astype(np.uint8).reshape(k // 512, 16, n))


def unpack_weight(words, scales, fmt):
    g, _, n = scales.shape
    words = np.ascontiguousarray(words).reshape(g, 128, n, -1)
    if fmt == "e4m3":
        vals = words.view(ml_dtypes.float8_e4m3fn).astype(np.float64)
    else:
        nib = np.empty((g, 128, n, 4), np.uint8)
        nib[..., 0::2] = words & 0xF
        nib[..., 1::2] = words >> 4
        vals = E2M1[nib]
    vals = vals * np.repeat(np.exp2(scales.astype(np.float64) - 127.0), 8, axis=1)[..., None]
    return vals.transpose(0, 1, 3, 2).reshape(g * 512, n)


def softplus(v):
    return np.log(1.0 + np.exp(v))


D, K, R, T, I, Q, G = 512, 512, 512, 2048, 512, 128, 64


def setup_inputs():
    n = np.random.standard_normal
    idx3 = np.random.permutation(I)[:I]
    idx = np.random.permutation(T)[:I]
    fd = mx_kscale(D)
    fk = mx_kscale(K)
    fi = mx_kscale(I)
    keysp = pack_weight(n((D, T)) / fd[:, None], "e4m3")
    tabp = pack_weight(n((K, T)) / fk[:, None], "e4m3")
    return {
        "query": (n((D, Q)) * 0.6 / np.sqrt(D) * fd[:, None]).astype(np.float32),
        "keys_words": keysp[0],
        "keys_scales": keysp[1],
        "sharp": (np.random.uniform(1.0, 3.0, (Q, 1))).astype(np.float32),
        "tab_words": tabp[0],
        "tab_scales": tabp[1],
        "w1": (n((K, R)) * 1 / np.sqrt(K) * fk[:, None]).astype(np.float32),
        "lam": (np.random.uniform(0.3, 1.0, (R, 1))).astype(np.float32),
        "os": (np.random.uniform(4.0, 16.0, (1, I)) * fi).astype(np.float32),
        "vs": (np.random.uniform(0.5, 2.0, (1, I)) / fi).astype(np.float32),
        "offs3": striped(idx3),
        "offs": striped(idx),
    }


def reference(query, keys_words, keys_scales, sharp, tab_words, tab_scales, w1, lam, os, vs, offs3, offs):
    idx3 = unstriped(offs3)
    idx = unstriped(offs)
    keysu = unpack_weight(keys_words, keys_scales, "e4m3")
    tabu = unpack_weight(tab_words, tab_scales, "e4m3")
    queryq = mxq(f64(query), 0, "e4m3")
    keysidxg = keysu[:, idx]
    a = queryq.T @ keysidxg
    p = np.exp(a)
    s = p.reshape(Q, G, I // G).sum(axis=2)
    ms = a.reshape(Q, G, I // G).mean(axis=2) * f64(sharp)
    pg = np.exp(ms - np.max(ms, axis=1, keepdims=True))
    z = np.sum(pg, axis=1, keepdims=True)
    sh = pg / z / s
    rr = np.repeat(sh, I // G, axis=1)
    w = p * rr
    w1q = mxq(f64(w1), 0, "e4m3")
    tabidxg = tabu[:, idx]
    zh = w1q.T @ tabidxg
    ht = softplus(zh)
    hv = ht + ht[:, idx3] * f64(lam)
    wo1 = w * f64(os)
    wt1 = wo1.T
    hw = hv * f64(vs)
    ht1 = hw.T
    wt1q = mxq(wt1, 0, "e4m3")
    ht1q = mxq(ht1, 0, "e4m3")
    o = wt1q.T @ ht1q
    return o

@@ -1,0 +1,206 @@
+from contextlib import ExitStack
+
+import concourse.mybir as mybir
+from concourse.masks import make_identity
+
+D, K, R, T, I, Q, G = 512, 512, 512, 2048, 512, 128, 64
+FLOPS = 2 * Q * D * I + 2 * R * K * I + 2 * Q * I * R
+
+F32 = mybir.dt.float32
+BF16 = mybir.dt.bfloat16
+I32 = mybir.dt.int32
+U32 = mybir.dt.uint32
+U16 = mybir.dt.uint16
+U8 = mybir.dt.uint8
+FP8X4 = mybir.dt.float8_e4m3fn_x4
+ALU = mybir.AluOpType
+ACT = mybir.ActivationFunctionType
+AXIS = mybir.AxisListType
+
+P = 128
+PACK = 4
+GROUP = I // G
+TILES = R // P
+SPARE = 8
+TAB_ROW, KEYS_ROW = 0, 4
+
+
+def tile_attend_lrlent_bygroup_kernel(tc, query, keys_words, keys_scales, sharp, tab_words, tab_scales,
+                                       w1, lam, slot_factor, vs, offs3, offs, out):
+    nc = tc.nc
+    with ExitStack() as ctx:
+        sb = ctx.enter_context(tc.tile_pool(name="sb", bufs=1))
+        ps = ctx.enter_context(tc.psum_pool(name="ps", bufs=1))
+
+        def tile(name, shape, dtype, tag=None):
+            return sb.tile(shape, dtype, name=name, tag=tag or name, align_bytes=64)
+
+        def load_scale_rows(plane, scales, row):
+            for quad in range(4):
+                nc.sync.dma_start(
+                    out=plane[32 * quad + row : 32 * quad + row + 4, :].bitcast(I32),
+                    in_=scales[0, 4 * quad : 4 * quad + 4, :].bitcast(I32),
+                )
+
+        def interleave(copy, dst, src):
+            copy(
+                out=dst.rearrange("p (c i) t -> p c t i", i=4),
+                in_=src.rearrange("p t (c i) -> p c t i", i=4),
+            )
+
+        def quantise(name, grouped):
+            width = grouped.shape[1]
+            codes = tile(name + "_codes", [P, width], U32)
+            scales = tile(name + "_scales", [P, width], U8)
+            nc.vector.quantize_mx(out=codes[:].bitcast(FP8X4), scales=scales[:],
+                                  in_=grouped[:].rearrange("p c t -> p (c t)"))
+            return codes[:], scales[:]
+
+        def product(bank, stationary, moving):
+            nc.tensor.matmul_mx(out=bank, lhsT=stationary[0].bitcast(FP8X4), lhsT_scale=stationary[1],
+                                rhs=moving[0].bitcast(FP8X4), rhs_scale=moving[1], start=True, stop=True)
+
+        def gather_packed(name, words, plane, offsets, row):
+            got_scales = tile(name + "_got_scales", [P, I], U8)
+            got_words = tile(name + "_got_words", [P, I], U32)
+            nc.vector.tensor_copy(out=got_scales[:], in_=plane[:].indirect(offsets[:]))
+            nc.vector.tensor_copy(out=got_words[:], in_=words[:].bitcast(U32).indirect(offsets[:]))
+            return got_words[:], got_scales[row:P, :]
+
+        lam_t = tile("lam_t", [P, TILES], F32)
+        with nc.allow_non_contiguous_dma(reason="one factor a partition for each tile of hidden features"):
+            nc.scalar.dma_start(out=lam_t[:], in_=lam.rearrange("(j p) o -> p (j o)", p=P))
+        tab_plane = tile("tab_plane", [P, T], U8)
+        keys_plane = tile("keys_plane", [P, T], U8)
+        nc.vector.memset(tab_plane[:].bitcast(I32), 0)
+        nc.vector.memset(keys_plane[:].bitcast(I32), 0)
+        ident = tile("ident", [P, P], F32)
+        make_identity(nc, ident[:])
+
+        offs_t = sb.tile([P, I // 16], U16, name="offs_t")
+        nc.sync.dma_start(offs_t[:], offs)
+        w1_rows = w1.rearrange("(p t) r -> p t r", t=PACK)
+        w1_first = tile("w1_first", [P, PACK, P], F32)
+        nc.sync.dma_start(out=w1_first[:], in_=w1_rows[:, :, 0:P])
+        load_scale_rows(tab_plane, tab_scales, TAB_ROW)
+        tab_pool = tile("tab_pool", [P, T], I32)
+        nc.sync.dma_start(out=tab_pool[:], in_=tab_words[0].rearrange("p n t -> p (n t)").bitcast(I32))
+        w1_second = tile("w1_second", [P, PACK, P], F32)
+        nc.sync.dma_start(out=w1_second[:], in_=w1_rows[:, :, P : 2 * P])
+        w1_back = tile("w1_back", [P, PACK, 2 * P], F32)
+        nc.sync.dma_start(out=w1_back[:], in_=w1_rows[:, :, 2 * P : R])
+        query_raw = tile("query_raw", [P, PACK, Q], F32)
+        nc.sync.dma_start(out=query_raw[:], in_=query.rearrange("(p t) q -> p t q", t=PACK))
+        offs3_t = sb.tile([P, I // 16], U16, name="offs3_t")
+        nc.sync.dma_start(offs3_t[:], offs3)
+        load_scale_rows(keys_plane, keys_scales, KEYS_ROW)
+        keys_pool = tile("keys_pool", [P, T], I32)
+        nc.sync.dma_start(out=keys_pool[:], in_=keys_words[0].rearrange("p n t -> p (n t)").bitcast(I32))
+        w1_raw = [w1_first[:], w1_second[:], w1_back[:, :, 0:P], w1_back[:, :, P : 2 * P]]
+        sharp_t = tile("sharp_t", [P, 1], F32)
+        nc.sync.dma_start(out=sharp_t, in_=sharp)
+        vs_t = tile("vs_t", [P, PACK], F32)
+        os_t = tile("os_t", [P, PACK], F32)
+        nc.sync.dma_start(out=os_t[:], in_=slot_factor.rearrange("o (p t) -> (o p) t", t=PACK))
+        nc.sync.dma_start(out=vs_t[:], in_=vs.rearrange("o (p t) -> (o p) t", t=PACK))
+
+
+        lam_wide = [tile(f"lam_wide{j}", [P, I], F32) for j in range(TILES)]
+        for j in range(TILES):
+            nc.scalar.activation(out=lam_wide[j][:], in_=lam_t[:, j : j + 1].to_broadcast([P, I]), func=ACT.Copy)
+
+        tab_got = gather_packed("tab", tab_pool, tab_plane, offs_t, TAB_ROW)
+        banks = [ps.tile([P, I], F32, name=f"bank{j}") for j in range(TILES)]
+        mag = tile("mag", [P, TILES * I], F32)
+        dec = tile("dec", [P, TILES * I], F32)
+        for j in range(TILES):
+            w1_grouped = tile(f"w1_grouped{j}", [P, P, PACK], BF16)
+            interleave(nc.scalar.copy if j == 1 else nc.vector.tensor_copy, w1_grouped[:], w1_raw[j])
+            product(banks[j][:], quantise(f"w1_{j}", w1_grouped), tab_got)
+            nc.scalar.activation(out=mag[:, j * I : (j + 1) * I], in_=banks[j][:], func=ACT.Abs)
+        nc.scalar.activation(out=dec[:], in_=mag[:], func=ACT.Exp, scale=-1.0)
+
+        keys_got = gather_packed("keys", keys_pool, keys_plane, offs_t, KEYS_ROW)
+        query_grouped = tile("query_grouped", [P, Q, PACK], BF16)
+        interleave(nc.vector.tensor_copy, query_grouped[:], query_raw[:])
+        score_bank = ps.tile([P, I], F32, name="score_bank")
+        product(score_bank[:], quantise("query", query_grouped), keys_got)
+        scores = score_bank[:].rearrange("p (g e) -> p g e", e=GROUP)
+        top = tile("top", [P, G], F32)
+        shifted = tile("shifted", [P, I], F32)
+        total = tile("total", [P, G], F32)
+        neg_sharp = tile("neg_sharp", [P, 1], F32)
+        neg_ms = tile("neg_ms", [P, G], F32)
+        neg_top_ms = tile("neg_top_ms", [P, 1], F32)
+
+        def dealt(ap):
+            return ap.rearrange("p (t g h) -> p t g h", t=PACK, g=G)
+
+        def per_group(ap):
+            return ap.unsqueeze(1).unsqueeze(3).to_broadcast([P, PACK, G, GROUP // PACK])
+
+        nc.vector.tensor_reduce(out=top[:], in_=scores, axis=AXIS.X, op=ALU.max)
+        nc.vector.tensor_tensor(out=dealt(shifted[:]),
+                                in0=score_bank[:].rearrange("p (g h t) -> p t g h", g=G, t=PACK),
+                                in1=per_group(top[:]), op=ALU.subtract)
+        nc.vector.tensor_reduce(out=total[:], in_=scores, axis=AXIS.X, op=ALU.add)
+        nc.gpsimd.tensor_scalar(out=neg_sharp[:], in0=sharp_t, scalar1=-1.0 / GROUP, scalar2=0.0,
+                                op0=ALU.mult, op1=ALU.add)
+        nc.vector.tensor_scalar(out=neg_ms[:], in0=total[:], scalar1=neg_sharp[:], scalar2=None,
+                                op0=ALU.mult, op1=ALU.min, accum_out=neg_top_ms[:])
+
+        score_operands = ["keys_got_words", "keys_got_scales", "query_codes", "query_scales"]
+        ht = [tile(f"ht{j}", [P, I + SPARE], F32, tag=score_operands[j]) for j in range(TILES)]
+        for j in range(TILES):
+            nc.gpsimd.memset(ht[j][:, I : I + SPARE], 0.0)
+        for j in range(TILES):
+            tail = mag[:, j * I : (j + 1) * I]
+            nc.scalar.activation(out=tail, in_=dec[:, j * I : (j + 1) * I], func=ACT.Ln, bias=1.0)
+            nc.vector.scalar_tensor_tensor(out=ht[j][:, 0:I], in0=banks[j][:], scalar=0.0, in1=tail,
+                                           op0=ALU.max, op1=ALU.add)
+            linked = tile(f"linked{j}", [P, I], F32)
+            nc.vector.tensor_tensor(out=linked[:], in0=ht[j][:].indirect(offs3_t[:]), in1=lam_wide[j][:], op=ALU.mult)
+            for n, term in enumerate((ht[j], linked)):
+                for t in range(PACK):
+                    nc.tensor.matmul(out=banks[j][:, t * P : (t + 1) * P], lhsT=term[:, t:I:PACK], rhs=ident[:],
+                                     is_transpose=True, start=(n == 0 and t == 0), stop=(n == 1 and t == PACK - 1))
+
+        p_t = dec[:, (TILES - 1) * I : TILES * I]
+        nc.scalar.activation(out=p_t, in_=shifted[:], func=ACT.Exp)
+        pg = shifted[:, 0:G]
+        z = tile("z", [P, 1], F32)
+        nc.scalar.activation(out=pg, in_=neg_ms[:], func=ACT.Exp, scale=-1.0, bias=neg_top_ms[:], accum_out=z[:])
+        s = tile("s", [P, G], F32)
+        sz = tile("sz", [P, G], F32)
+        rec = tile("rec", [P, G], F32)
+        sh = tile("sh", [P, G], F32)
+        w = tile("w", [P, I], F32)
+        nc.vector.tensor_reduce(out=s[:], in_=p_t.rearrange("p (t g h) -> p g t h", t=PACK, g=G),
+                                axis=AXIS.XY, op=ALU.add)
+        nc.vector.tensor_scalar(out=sz[:], in0=s[:], scalar1=z[:], scalar2=None, op0=ALU.mult)
+        nc.vector.reciprocal(out=rec[:], in_=sz[:])
+        nc.vector.tensor_tensor(out=sh[:], in0=pg, in1=rec[:], op=ALU.mult)
+        nc.vector.tensor_tensor(out=dealt(w[:]), in0=dealt(p_t), in1=per_group(sh[:]), op=ALU.mult)
+        for t in range(PACK):
+            nc.tensor.transpose(score_bank[:, t * P : (t + 1) * P], w[:, t * P : (t + 1) * P], ident[:])
+        wt1 = tile("wt1", [P, Q, PACK], BF16)
+        nc.vector.tensor_tensor(out=wt1[:], in0=score_bank[:].rearrange("p (t c) -> p c t", t=PACK),
+                                in1=os_t[:].unsqueeze(1).to_broadcast([P, Q, PACK]), op=ALU.mult)
+        weights = quantise("wt1", wt1)
+
+        for half in range(2):
+            ht1 = tile(f"ht1_{half}", [P, 2 * P, PACK], BF16)
+            for n in range(2):
+                j = 2 * half + n
+                planes = tile(f"planes{j}", [P, PACK, P], BF16)
+                for t in range(PACK):
+                    nc.scalar.activation(out=planes[:, t, :], in_=banks[j][:, t * P : (t + 1) * P], func=ACT.Copy,
+                                         scale=vs_t[:, t : t + 1])
+                interleave(nc.scalar.copy, ht1[:, n * P : (n + 1) * P, :], planes[:])
+            out_bank = ps.tile([P, I], F32, name=f"out_bank{half}")
+            product(out_bank[:, 0 : 2 * P], weights, quantise(f"ht1_{half}", ht1))
+            result = tile(f"result{half}", [P, 2 * P], F32)
+            copy = nc.scalar.copy if half == 0 else nc.vector.tensor_copy
+            copy(out=result[:], in_=out_bank[:, 0 : 2 * P])
+            queue = nc.scalar if half == 0 else nc.sync
+            queue.dma_start(out=out[:, half * 2 * P : (half + 1) * 2 * P], in_=result[:])

@@ -91,26 +91,26 @@ def tile_attend_lrlent_bygroup_kernel(tc, query, keys_words, keys_scales, sharp,
         nc.sync.dma_start(out=w1_back[:], in_=w1_rows[:, :, 2 * P : R])
         query_raw = tile("query_raw", [P, PACK, Q], F32)
         nc.sync.dma_start(out=query_raw[:], in_=query.rearrange("(p t) q -> p t q", t=PACK))
-        offs3_t = sb.tile([P, I // 16], U16, name="offs3_t")
-        nc.sync.dma_start(offs3_t[:], offs3)
         load_scale_rows(keys_plane, keys_scales, KEYS_ROW)
         keys_pool = tile("keys_pool", [P, T], I32)
         nc.sync.dma_start(out=keys_pool[:], in_=keys_words[0].rearrange("p n t -> p (n t)").bitcast(I32))
         w1_raw = [w1_first[:], w1_second[:], w1_back[:, :, 0:P], w1_back[:, :, P : 2 * P]]
         sharp_t = tile("sharp_t", [P, 1], F32)
-        nc.sync.dma_start(out=sharp_t, in_=sharp)
+        nc.sync.dma_start(out=sharp_t[:], in_=sharp)
+        offs3_t = sb.tile([P, I // 16], U16, name="offs3_t")
+        nc.sync.dma_start(offs3_t[:], offs3)
         vs_t = tile("vs_t", [P, PACK], F32)
         os_t = tile("os_t", [P, PACK], F32)
         nc.sync.dma_start(out=os_t[:], in_=slot_factor.rearrange("o (p t) -> (o p) t", t=PACK))
         nc.sync.dma_start(out=vs_t[:], in_=vs.rearrange("o (p t) -> (o p) t", t=PACK))
 
 
+        banks = [ps.tile([P, I], F32, name=f"bank{j}") for j in range(TILES)]
         lam_wide = [tile(f"lam_wide{j}", [P, I], F32) for j in range(TILES)]
         for j in range(TILES):
             nc.scalar.activation(out=lam_wide[j][:], in_=lam_t[:, j : j + 1].to_broadcast([P, I]), func=ACT.Copy)
 
         tab_got = gather_packed("tab", tab_pool, tab_plane, offs_t, TAB_ROW)
-        banks = [ps.tile([P, I], F32, name=f"bank{j}") for j in range(TILES)]
         mag = tile("mag", [P, TILES * I], F32)
         dec = tile("dec", [P, TILES * I], F32)
         for j in range(TILES):
@@ -144,7 +144,7 @@ def tile_attend_lrlent_bygroup_kernel(tc, query, keys_words, keys_scales, sharp,
                                 in0=score_bank[:].rearrange("p (g h t) -> p t g h", g=G, t=PACK),
                                 in1=per_group(top[:]), op=ALU.subtract)
         nc.vector.tensor_reduce(out=total[:], in_=scores, axis=AXIS.X, op=ALU.add)
-        nc.gpsimd.tensor_scalar(out=neg_sharp[:], in0=sharp_t, scalar1=-1.0 / GROUP, scalar2=0.0,
+        nc.gpsimd.tensor_scalar(out=neg_sharp[:], in0=sharp_t[:], scalar1=-1.0 / GROUP, scalar2=0.0,
                                 op0=ALU.mult, op1=ALU.add)
         nc.vector.tensor_scalar(out=neg_ms[:], in0=total[:], scalar1=neg_sharp[:], scalar2=None,
                                 op0=ALU.mult, op1=ALU.min, accum_out=neg_top_ms[:])
@@ -153,17 +153,25 @@ def tile_attend_lrlent_bygroup_kernel(tc, query, keys_words, keys_scales, sharp,
         ht = [tile(f"ht{j}", [P, I + SPARE], F32, tag=score_operands[j]) for j in range(TILES)]
         for j in range(TILES):
             nc.gpsimd.memset(ht[j][:, I : I + SPARE], 0.0)
+
+        def turn(j, term, first):
+            for t in range(PACK):
+                nc.tensor.matmul(out=banks[j][:, t * P : (t + 1) * P], lhsT=term[:, t:I:PACK], rhs=ident[:],
+                                 is_transpose=True, start=(first and t == 0), stop=(not first and t == PACK - 1))
+
+        def link(j, tag):
+            linked = tile(f"linked{j}", [P, I], F32, tag=tag)
+            nc.vector.tensor_tensor(out=linked[:], in0=ht[j][:].indirect(offs3_t[:]), in1=lam_wide[j][:], op=ALU.mult)
+            turn(j, linked, first=False)
+
         for j in range(TILES):
             tail = mag[:, j * I : (j + 1) * I]
             nc.scalar.activation(out=tail, in_=dec[:, j * I : (j + 1) * I], func=ACT.Ln, bias=1.0)
             nc.vector.scalar_tensor_tensor(out=ht[j][:, 0:I], in0=banks[j][:], scalar=0.0, in1=tail,
                                            op0=ALU.max, op1=ALU.add)
-            linked = tile(f"linked{j}", [P, I], F32)
-            nc.vector.tensor_tensor(out=linked[:], in0=ht[j][:].indirect(offs3_t[:]), in1=lam_wide[j][:], op=ALU.mult)
-            for n, term in enumerate((ht[j], linked)):
-                for t in range(PACK):
-                    nc.tensor.matmul(out=banks[j][:, t * P : (t + 1) * P], lhsT=term[:, t:I:PACK], rhs=ident[:],
-                                     is_transpose=True, start=(n == 0 and t == 0), stop=(n == 1 and t == PACK - 1))
+            turn(j, ht[j], first=True)
+            if j < 2:
+                link(j, None)
 
         p_t = dec[:, (TILES - 1) * I : TILES * I]
         nc.scalar.activation(out=p_t, in_=shifted[:], func=ACT.Exp)
@@ -171,36 +179,51 @@ def tile_attend_lrlent_bygroup_kernel(tc, query, keys_words, keys_scales, sharp,
         z = tile("z", [P, 1], F32)
         nc.scalar.activation(out=pg, in_=neg_ms[:], func=ACT.Exp, scale=-1.0, bias=neg_top_ms[:], accum_out=z[:])
         s = tile("s", [P, G], F32)
-        sz = tile("sz", [P, G], F32)
-        rec = tile("rec", [P, G], F32)
+        inv_z = tile("inv_z", [P, 1], F32)
+        inv_s = tile("inv_s", [P, G], F32)
         sh = tile("sh", [P, G], F32)
         w = tile("w", [P, I], F32)
         nc.vector.tensor_reduce(out=s[:], in_=p_t.rearrange("p (t g h) -> p g t h", t=PACK, g=G),
                                 axis=AXIS.XY, op=ALU.add)
-        nc.vector.tensor_scalar(out=sz[:], in0=s[:], scalar1=z[:], scalar2=None, op0=ALU.mult)
-        nc.vector.reciprocal(out=rec[:], in_=sz[:])
-        nc.vector.tensor_tensor(out=sh[:], in0=pg, in1=rec[:], op=ALU.mult)
+        nc.vector.reciprocal(out=inv_z[:], in_=z[:])
+        nc.vector.reciprocal(out=inv_s[:], in_=s[:])
+        link(2, "s")
+        nc.vector.scalar_tensor_tensor(out=sh[:], in0=pg, scalar=inv_z[:], in1=inv_s[:], op0=ALU.mult, op1=ALU.mult)
         nc.vector.tensor_tensor(out=dealt(w[:]), in0=dealt(p_t), in1=per_group(sh[:]), op=ALU.mult)
         for t in range(PACK):
             nc.tensor.transpose(score_bank[:, t * P : (t + 1) * P], w[:, t * P : (t + 1) * P], ident[:])
+        link(3, "sh")
+
+        def scale_on_vector(grouped, bank, factor):
+            nc.vector.tensor_tensor(out=grouped, in0=bank[:].rearrange("p (t c) -> p c t", t=PACK),
+                                    in1=factor[:].unsqueeze(1).to_broadcast([P, P, PACK]), op=ALU.mult)
+
+        def scale_on_scalar(grouped, bank, factor, name):
+            planes = tile(name, [P, PACK, P], BF16)
+            for t in range(PACK):
+                nc.scalar.activation(out=planes[:, t, :], in_=bank[:, t * P : (t + 1) * P], func=ACT.Copy,
+                                     scale=factor[:, t : t + 1])
+            interleave(nc.scalar.copy, grouped, planes[:])
+
         wt1 = tile("wt1", [P, Q, PACK], BF16)
-        nc.vector.tensor_tensor(out=wt1[:], in0=score_bank[:].rearrange("p (t c) -> p c t", t=PACK),
-                                in1=os_t[:].unsqueeze(1).to_broadcast([P, Q, PACK]), op=ALU.mult)
+        scale_on_vector(wt1[:], score_bank, os_t)
         weights = quantise("wt1", wt1)
 
-        for half in range(2):
-            ht1 = tile(f"ht1_{half}", [P, 2 * P, PACK], BF16)
-            for n in range(2):
-                j = 2 * half + n
-                planes = tile(f"planes{j}", [P, PACK, P], BF16)
-                for t in range(PACK):
-                    nc.scalar.activation(out=planes[:, t, :], in_=banks[j][:, t * P : (t + 1) * P], func=ACT.Copy,
-                                         scale=vs_t[:, t : t + 1])
-                interleave(nc.scalar.copy, ht1[:, n * P : (n + 1) * P, :], planes[:])
-            out_bank = ps.tile([P, I], F32, name=f"out_bank{half}")
-            product(out_bank[:, 0 : 2 * P], weights, quantise(f"ht1_{half}", ht1))
-            result = tile(f"result{half}", [P, 2 * P], F32)
-            copy = nc.scalar.copy if half == 0 else nc.vector.tensor_copy
-            copy(out=result[:], in_=out_bank[:, 0 : 2 * P])
-            queue = nc.scalar if half == 0 else nc.sync
-            queue.dma_start(out=out[:, half * 2 * P : (half + 1) * 2 * P], in_=result[:])
+        ht1_front = tile("ht1_front", [P, 2 * P, PACK], BF16)
+        ht1_third = tile("ht1_third", [P, P, PACK], BF16)
+        ht1_last = tile("ht1_last", [P, P, PACK], BF16)
+        scale_on_scalar(ht1_front[:, 0:P, :], banks[0], vs_t, "planes0")
+        scale_on_scalar(ht1_front[:, P : 2 * P, :], banks[1], vs_t, "planes1")
+        scale_on_scalar(ht1_third[:], banks[2], vs_t, "planes2")
+        early_bank = ps.tile([P, I], F32, name="early_bank")
+        product(early_bank[:, 0 : 2 * P], weights, quantise("ht1_front", ht1_front))
+        product(early_bank[:, 2 * P : 3 * P], weights, quantise("ht1_third", ht1_third))
+        early = tile("early", [P, 3 * P], F32)
+        nc.scalar.copy(out=early[:], in_=early_bank[:, 0 : 3 * P])
+        nc.scalar.dma_start(out=out[:, 0 : 3 * P], in_=early[:])
+        scale_on_vector(ht1_last[:], banks[3], vs_t)
+        late_bank = ps.tile([P, I], F32, name="late_bank")
+        product(late_bank[:, 0:P], weights, quantise("ht1_last", ht1_last))
+        late = tile("late", [P, P], F32)
+        nc.vector.tensor_copy(out=late[:], in_=late_bank[:, 0:P])
+        nc.sync.dma_start(out=out[:, 3 * P : R], in_=late[:])

@@ -35,12 +35,9 @@ def tile_attend_lrlent_bygroup_kernel(tc, query, keys_words, keys_scales, sharp,
         def tile(name, shape, dtype, tag=None):
             return sb.tile(shape, dtype, name=name, tag=tag or name, align_bytes=64)
 
-        def load_scale_rows(plane, scales, row):
-            for quad in range(4):
-                nc.sync.dma_start(
-                    out=plane[32 * quad + row : 32 * quad + row + 4, :].bitcast(I32),
-                    in_=scales[0, 4 * quad : 4 * quad + 4, :].bitcast(I32),
-                )
+        def load_scale_rows(queue, plane, scales, row):
+            for f in range(4):
+                queue.dma_start(out=plane[row + f : P : 32, :].bitcast(I32), in_=scales[0, f:16:4, :].bitcast(I32))
 
         def interleave(copy, dst, src):
             copy(
@@ -73,7 +70,8 @@ def tile_attend_lrlent_bygroup_kernel(tc, query, keys_words, keys_scales, sharp,
         tab_plane = tile("tab_plane", [P, T], U8)
         keys_plane = tile("keys_plane", [P, T], U8)
         nc.vector.memset(tab_plane[:].bitcast(I32), 0)
-        nc.vector.memset(keys_plane[:].bitcast(I32), 0)
+        nc.gpsimd.memset(keys_plane[:].bitcast(I32), 0)
+        load_scale_rows(nc.gpsimd, keys_plane, keys_scales, KEYS_ROW)
         ident = tile("ident", [P, P], F32)
         make_identity(nc, ident[:])
 
@@ -82,7 +80,7 @@ def tile_attend_lrlent_bygroup_kernel(tc, query, keys_words, keys_scales, sharp,
         w1_rows = w1.rearrange("(p t) r -> p t r", t=PACK)
         w1_first = tile("w1_first", [P, PACK, P], F32)
         nc.sync.dma_start(out=w1_first[:], in_=w1_rows[:, :, 0:P])
-        load_scale_rows(tab_plane, tab_scales, TAB_ROW)
+        load_scale_rows(nc.sync, tab_plane, tab_scales, TAB_ROW)
         tab_pool = tile("tab_pool", [P, T], I32)
         nc.sync.dma_start(out=tab_pool[:], in_=tab_words[0].rearrange("p n t -> p (n t)").bitcast(I32))
         w1_second = tile("w1_second", [P, PACK, P], F32)
@@ -91,7 +89,6 @@ def tile_attend_lrlent_bygroup_kernel(tc, query, keys_words, keys_scales, sharp,
         nc.sync.dma_start(out=w1_back[:], in_=w1_rows[:, :, 2 * P : R])
         query_raw = tile("query_raw", [P, PACK, Q], F32)
         nc.sync.dma_start(out=query_raw[:], in_=query.rearrange("(p t) q -> p t q", t=PACK))
-        load_scale_rows(keys_plane, keys_scales, KEYS_ROW)
         keys_pool = tile("keys_pool", [P, T], I32)
         nc.sync.dma_start(out=keys_pool[:], in_=keys_words[0].rearrange("p n t -> p (n t)").bitcast(I32))
         w1_raw = [w1_first[:], w1_second[:], w1_back[:, :, 0:P], w1_back[:, :, P : 2 * P]]
@@ -114,7 +111,7 @@ def tile_attend_lrlent_bygroup_kernel(tc, query, keys_words, keys_scales, sharp,
         mag = tile("mag", [P, TILES * I], F32)
         dec = tile("dec", [P, TILES * I], F32)
         for j in range(TILES):
-            w1_grouped = tile(f"w1_grouped{j}", [P, P, PACK], BF16)
+            w1_grouped = tile(f"w1_grouped{j}", [P, P, PACK], BF16, tag="keys_got_scales" if j == TILES - 1 else None)
             interleave(nc.scalar.copy if j == 1 else nc.vector.tensor_copy, w1_grouped[:], w1_raw[j])
             product(banks[j][:], quantise(f"w1_{j}", w1_grouped), tab_got)
             nc.scalar.activation(out=mag[:, j * I : (j + 1) * I], in_=banks[j][:], func=ACT.Abs)

@@ -22,6 +22,7 @@ PACK = 4
 GROUP = I // G
 TILES = R // P
 SPARE = 8
+LAM_PITCH = 8
 TAB_ROW, KEYS_ROW = 0, 4
 
 
@@ -64,9 +65,9 @@ def tile_attend_lrlent_bygroup_kernel(tc, query, keys_words, keys_scales, sharp,
             nc.vector.tensor_copy(out=got_words[:], in_=words[:].bitcast(U32).indirect(offsets[:]))
             return got_words[:], got_scales[row:P, :]
 
-        lam_t = tile("lam_t", [P, TILES], F32)
+        lam_t = tile("lam_t", [P, TILES, LAM_PITCH], F32)
         with nc.allow_non_contiguous_dma(reason="one factor a partition for each tile of hidden features"):
-            nc.scalar.dma_start(out=lam_t[:], in_=lam.rearrange("(j p) o -> p (j o)", p=P))
+            nc.scalar.dma_start(out=lam_t[:, :, 0:1], in_=lam.rearrange("(j p) o -> p j o", p=P))
         tab_plane = tile("tab_plane", [P, T], U8)
         keys_plane = tile("keys_plane", [P, T], U8)
         nc.vector.memset(tab_plane[:].bitcast(I32), 0)
@@ -105,7 +106,7 @@ def tile_attend_lrlent_bygroup_kernel(tc, query, keys_words, keys_scales, sharp,
         banks = [ps.tile([P, I], F32, name=f"bank{j}") for j in range(TILES)]
         lam_wide = [tile(f"lam_wide{j}", [P, I], F32) for j in range(TILES)]
         for j in range(TILES):
-            nc.scalar.activation(out=lam_wide[j][:], in_=lam_t[:, j : j + 1].to_broadcast([P, I]), func=ACT.Copy)
+            nc.scalar.activation(out=lam_wide[j][:], in_=lam_t[:, j, 0:1].to_broadcast([P, I]), func=ACT.Copy)
 
         tab_got = gather_packed("tab", tab_pool, tab_plane, offs_t, TAB_ROW)
         mag = tile("mag", [P, TILES * I], F32)

from contextlib import ExitStack

import concourse.mybir as mybir
from concourse.masks import make_identity

D, K, R, T, I, Q, G = 512, 512, 512, 2048, 512, 128, 64
FLOPS = 2 * Q * D * I + 2 * R * K * I + 2 * Q * I * R

F32 = mybir.dt.float32
BF16 = mybir.dt.bfloat16
I32 = mybir.dt.int32
U32 = mybir.dt.uint32
U16 = mybir.dt.uint16
U8 = mybir.dt.uint8
FP8X4 = mybir.dt.float8_e4m3fn_x4
ALU = mybir.AluOpType
ACT = mybir.ActivationFunctionType
AXIS = mybir.AxisListType

P = 128
PACK = 4
GROUP = I // G
TILES = R // P
SPARE = 8
LAM_PITCH = 8
TAB_ROW, KEYS_ROW = 0, 4


def tile_attend_lrlent_bygroup_kernel(tc, query, keys_words, keys_scales, sharp, tab_words, tab_scales,
                                       w1, lam, slot_factor, vs, offs3, offs, out):
    nc = tc.nc
    with ExitStack() as ctx:
        sb = ctx.enter_context(tc.tile_pool(name="sb", bufs=1))
        ps = ctx.enter_context(tc.psum_pool(name="ps", bufs=1))

        def tile(name, shape, dtype, tag=None):
            return sb.tile(shape, dtype, name=name, tag=tag or name, align_bytes=64)

        def load_scale_rows(queue, plane, scales, row):
            for f in range(4):
                queue.dma_start(out=plane[row + f : P : 32, :].bitcast(I32), in_=scales[0, f:16:4, :].bitcast(I32))

        def interleave(copy, dst, src):
            copy(
                out=dst.rearrange("p (c i) t -> p c t i", i=4),
                in_=src.rearrange("p t (c i) -> p c t i", i=4),
            )

        def quantise(name, grouped):
            width = grouped.shape[1]
            codes = tile(name + "_codes", [P, width], U32)
            scales = tile(name + "_scales", [P, width], U8)
            nc.vector.quantize_mx(out=codes[:].bitcast(FP8X4), scales=scales[:],
                                  in_=grouped[:].rearrange("p c t -> p (c t)"))
            return codes[:], scales[:]

        def product(bank, stationary, moving):
            nc.tensor.matmul_mx(out=bank, lhsT=stationary[0].bitcast(FP8X4), lhsT_scale=stationary[1],
                                rhs=moving[0].bitcast(FP8X4), rhs_scale=moving[1], start=True, stop=True)

        def gather_packed(name, words, plane, offsets, row):
            got_scales = tile(name + "_got_scales", [P, I], U8)
            got_words = tile(name + "_got_words", [P, I], U32)
            nc.vector.tensor_copy(out=got_scales[:], in_=plane[:].indirect(offsets[:]))
            nc.vector.tensor_copy(out=got_words[:], in_=words[:].bitcast(U32).indirect(offsets[:]))
            return got_words[:], got_scales[row:P, :]

        lam_t = tile("lam_t", [P, TILES, LAM_PITCH], F32)
        with nc.allow_non_contiguous_dma(reason="one factor a partition for each tile of hidden features"):
            nc.scalar.dma_start(out=lam_t[:, :, 0:1], in_=lam.rearrange("(j p) o -> p j o", p=P))
        tab_plane = tile("tab_plane", [P, T], U8)
        keys_plane = tile("keys_plane", [P, T], U8)
        nc.vector.memset(tab_plane[:].bitcast(I32), 0)
        nc.gpsimd.memset(keys_plane[:].bitcast(I32), 0)
        load_scale_rows(nc.gpsimd, keys_plane, keys_scales, KEYS_ROW)
        ident = tile("ident", [P, P], F32)
        make_identity(nc, ident[:])

        offs_t = sb.tile([P, I // 16], U16, name="offs_t")
        nc.sync.dma_start(offs_t[:], offs)
        w1_rows = w1.rearrange("(p t) r -> p t r", t=PACK)
        w1_first = tile("w1_first", [P, PACK, P], F32)
        nc.sync.dma_start(out=w1_first[:], in_=w1_rows[:, :, 0:P])
        load_scale_rows(nc.sync, tab_plane, tab_scales, TAB_ROW)
        tab_pool = tile("tab_pool", [P, T], I32)
        nc.sync.dma_start(out=tab_pool[:], in_=tab_words[0].rearrange("p n t -> p (n t)").bitcast(I32))
        w1_second = tile("w1_second", [P, PACK, P], F32)
        nc.sync.dma_start(out=w1_second[:], in_=w1_rows[:, :, P : 2 * P])
        w1_back = tile("w1_back", [P, PACK, 2 * P], F32)
        nc.sync.dma_start(out=w1_back[:], in_=w1_rows[:, :, 2 * P : R])
        query_raw = tile("query_raw", [P, PACK, Q], F32)
        nc.sync.dma_start(out=query_raw[:], in_=query.rearrange("(p t) q -> p t q", t=PACK))
        keys_pool = tile("keys_pool", [P, T], I32)
        nc.sync.dma_start(out=keys_pool[:], in_=keys_words[0].rearrange("p n t -> p (n t)").bitcast(I32))
        w1_raw = [w1_first[:], w1_second[:], w1_back[:, :, 0:P], w1_back[:, :, P : 2 * P]]
        sharp_t = tile("sharp_t", [P, 1], F32)
        nc.sync.dma_start(out=sharp_t[:], in_=sharp)
        offs3_t = sb.tile([P, I // 16], U16, name="offs3_t")
        nc.sync.dma_start(offs3_t[:], offs3)
        vs_t = tile("vs_t", [P, PACK], F32)
        os_t = tile("os_t", [P, PACK], F32)
        nc.sync.dma_start(out=os_t[:], in_=slot_factor.rearrange("o (p t) -> (o p) t", t=PACK))
        nc.sync.dma_start(out=vs_t[:], in_=vs.rearrange("o (p t) -> (o p) t", t=PACK))


        banks = [ps.tile([P, I], F32, name=f"bank{j}") for j in range(TILES)]
        lam_wide = [tile(f"lam_wide{j}", [P, I], F32) for j in range(TILES)]
        for j in range(TILES):
            nc.scalar.activation(out=lam_wide[j][:], in_=lam_t[:, j, 0:1].to_broadcast([P, I]), func=ACT.Copy)

        tab_got = gather_packed("tab", tab_pool, tab_plane, offs_t, TAB_ROW)
        mag = tile("mag", [P, TILES * I], F32)
        dec = tile("dec", [P, TILES * I], F32)
        for j in range(TILES):
            w1_grouped = tile(f"w1_grouped{j}", [P, P, PACK], BF16, tag="keys_got_scales" if j == TILES - 1 else None)
            interleave(nc.scalar.copy if j == 1 else nc.vector.tensor_copy, w1_grouped[:], w1_raw[j])
            product(banks[j][:], quantise(f"w1_{j}", w1_grouped), tab_got)
            nc.scalar.activation(out=mag[:, j * I : (j + 1) * I], in_=banks[j][:], func=ACT.Abs)
        nc.scalar.activation(out=dec[:], in_=mag[:], func=ACT.Exp, scale=-1.0)

        keys_got = gather_packed("keys", keys_pool, keys_plane, offs_t, KEYS_ROW)
        query_grouped = tile("query_grouped", [P, Q, PACK], BF16)
        interleave(nc.vector.tensor_copy, query_grouped[:], query_raw[:])
        score_bank = ps.tile([P, I], F32, name="score_bank")
        product(score_bank[:], quantise("query", query_grouped), keys_got)
        scores = score_bank[:].rearrange("p (g e) -> p g e", e=GROUP)
        top = tile("top", [P, G], F32)
        shifted = tile("shifted", [P, I], F32)
        total = tile("total", [P, G], F32)
        neg_sharp = tile("neg_sharp", [P, 1], F32)
        neg_ms = tile("neg_ms", [P, G], F32)
        neg_top_ms = tile("neg_top_ms", [P, 1], F32)

        def dealt(ap):
            return ap.rearrange("p (t g h) -> p t g h", t=PACK, g=G)

        def per_group(ap):
            return ap.unsqueeze(1).unsqueeze(3).to_broadcast([P, PACK, G, GROUP // PACK])

        nc.vector.tensor_reduce(out=top[:], in_=scores, axis=AXIS.X, op=ALU.max)
        nc.vector.tensor_tensor(out=dealt(shifted[:]),
                                in0=score_bank[:].rearrange("p (g h t) -> p t g h", g=G, t=PACK),
                                in1=per_group(top[:]), op=ALU.subtract)
        nc.vector.tensor_reduce(out=total[:], in_=scores, axis=AXIS.X, op=ALU.add)
        nc.gpsimd.tensor_scalar(out=neg_sharp[:], in0=sharp_t[:], scalar1=-1.0 / GROUP, scalar2=0.0,
                                op0=ALU.mult, op1=ALU.add)
        nc.vector.tensor_scalar(out=neg_ms[:], in0=total[:], scalar1=neg_sharp[:], scalar2=None,
                                op0=ALU.mult, op1=ALU.min, accum_out=neg_top_ms[:])

        score_operands = ["keys_got_words", "keys_got_scales", "query_codes", "query_scales"]
        ht = [tile(f"ht{j}", [P, I + SPARE], F32, tag=score_operands[j]) for j in range(TILES)]
        for j in range(TILES):
            nc.gpsimd.memset(ht[j][:, I : I + SPARE], 0.0)

        def turn(j, term, first):
            for t in range(PACK):
                nc.tensor.matmul(out=banks[j][:, t * P : (t + 1) * P], lhsT=term[:, t:I:PACK], rhs=ident[:],
                                 is_transpose=True, start=(first and t == 0), stop=(not first and t == PACK - 1))

        def link(j, tag):
            linked = tile(f"linked{j}", [P, I], F32, tag=tag)
            nc.vector.tensor_tensor(out=linked[:], in0=ht[j][:].indirect(offs3_t[:]), in1=lam_wide[j][:], op=ALU.mult)
            turn(j, linked, first=False)

        for j in range(TILES):
            tail = mag[:, j * I : (j + 1) * I]
            nc.scalar.activation(out=tail, in_=dec[:, j * I : (j + 1) * I], func=ACT.Ln, bias=1.0)
            nc.vector.scalar_tensor_tensor(out=ht[j][:, 0:I], in0=banks[j][:], scalar=0.0, in1=tail,
                                           op0=ALU.max, op1=ALU.add)
            turn(j, ht[j], first=True)
            if j < 2:
                link(j, None)

        p_t = dec[:, (TILES - 1) * I : TILES * I]
        nc.scalar.activation(out=p_t, in_=shifted[:], func=ACT.Exp)
        pg = shifted[:, 0:G]
        z = tile("z", [P, 1], F32)
        nc.scalar.activation(out=pg, in_=neg_ms[:], func=ACT.Exp, scale=-1.0, bias=neg_top_ms[:], accum_out=z[:])
        s = tile("s", [P, G], F32)
        inv_z = tile("inv_z", [P, 1], F32)
        inv_s = tile("inv_s", [P, G], F32)
        sh = tile("sh", [P, G], F32)
        w = tile("w", [P, I], F32)
        nc.vector.tensor_reduce(out=s[:], in_=p_t.rearrange("p (t g h) -> p g t h", t=PACK, g=G),
                                axis=AXIS.XY, op=ALU.add)
        nc.vector.reciprocal(out=inv_z[:], in_=z[:])
        nc.vector.reciprocal(out=inv_s[:], in_=s[:])
        link(2, "s")
        nc.vector.scalar_tensor_tensor(out=sh[:], in0=pg, scalar=inv_z[:], in1=inv_s[:], op0=ALU.mult, op1=ALU.mult)
        nc.vector.tensor_tensor(out=dealt(w[:]), in0=dealt(p_t), in1=per_group(sh[:]), op=ALU.mult)
        for t in range(PACK):
            nc.tensor.transpose(score_bank[:, t * P : (t + 1) * P], w[:, t * P : (t + 1) * P], ident[:])
        link(3, "sh")

        def scale_on_vector(grouped, bank, factor):
            nc.vector.tensor_tensor(out=grouped, in0=bank[:].rearrange("p (t c) -> p c t", t=PACK),
                                    in1=factor[:].unsqueeze(1).to_broadcast([P, P, PACK]), op=ALU.mult)

        def scale_on_scalar(grouped, bank, factor, name):
            planes = tile(name, [P, PACK, P], BF16)
            for t in range(PACK):
                nc.scalar.activation(out=planes[:, t, :], in_=bank[:, t * P : (t + 1) * P], func=ACT.Copy,
                                     scale=factor[:, t : t + 1])
            interleave(nc.scalar.copy, grouped, planes[:])

        wt1 = tile("wt1", [P, Q, PACK], BF16)
        scale_on_vector(wt1[:], score_bank, os_t)
        weights = quantise("wt1", wt1)

        ht1_front = tile("ht1_front", [P, 2 * P, PACK], BF16)
        ht1_third = tile("ht1_third", [P, P, PACK], BF16)
        ht1_last = tile("ht1_last", [P, P, PACK], BF16)
        scale_on_scalar(ht1_front[:, 0:P, :], banks[0], vs_t, "planes0")
        scale_on_scalar(ht1_front[:, P : 2 * P, :], banks[1], vs_t, "planes1")
        scale_on_scalar(ht1_third[:], banks[2], vs_t, "planes2")
        early_bank = ps.tile([P, I], F32, name="early_bank")
        product(early_bank[:, 0 : 2 * P], weights, quantise("ht1_front", ht1_front))
        product(early_bank[:, 2 * P : 3 * P], weights, quantise("ht1_third", ht1_third))
        early = tile("early", [P, 3 * P], F32)
        nc.scalar.copy(out=early[:], in_=early_bank[:, 0 : 3 * P])
        nc.scalar.dma_start(out=out[:, 0 : 3 * P], in_=early[:])
        scale_on_vector(ht1_last[:], banks[3], vs_t)
        late_bank = ps.tile([P, I], F32, name="late_bank")
        product(late_bank[:, 0:P], weights, quantise("ht1_last", ht1_last))
        late = tile("late", [P, P], F32)
        nc.vector.tensor_copy(out=late[:], in_=late_bank[:, 0:P])
        nc.sync.dma_start(out=out[:, 3 * P : R], in_=late[:])
